import numpy as np
import ml_dtypes


def mxq(x, axis, fmt="e4m3"):
    dtype, down = {"e4m3": (ml_dtypes.float8_e4m3fn, 7), "e5m2": (ml_dtypes.float8_e5m2, 14)}[fmt]
    v = np.moveaxis(np.asarray(x, np.float32).astype(ml_dtypes.bfloat16).astype(np.float64), axis, -1)
    blocks = v.reshape(v.shape[:-1] + (-1, 32))
    amax = np.abs(blocks).max(-1, keepdims=True)
    byte = np.maximum(np.where(amax > 0, np.frexp(amax)[1] - 1 + 127, 0) - down, 1)
    scale = np.exp2(byte - 127.0)
    codes = (blocks / scale).astype(np.float32).astype(dtype).astype(np.float64)
    return np.moveaxis((codes * scale).reshape(v.shape), -1, axis)


WIDE = False


def mx_kscale(k):
    if not WIDE:
        return np.ones(k)
    levels = np.array([10, -10, 5, -5, 0])
    if k % 512:
        return np.exp2(np.random.permutation(np.resize(levels, k // 32))).repeat(32)
    a = np.empty((k // 512, 16))
    for p in range(k // 512):
        a[p, :8] = np.random.permutation(np.resize(levels, 8))
        for g in range(8):
            far = levels[np.abs(levels - a[p, g]) >= 10]
            a[p, g + 8] = far[np.random.randint(len(far))]
    return np.exp2(a.ravel()).repeat(32)


def f64(x):
    return np.asarray(x).astype(np.float64)


def striped(idx):
    return np.tile(idx.reshape(-1, 16).T, (8, 1)).astype(np.uint16)


def unstriped(offs):
    return offs[:16].T.reshape(-1).astype(np.int64)


def pack_weight(w):
    k, n = w.shape
    w = f64(np.asarray(w, np.float32).astype(ml_dtypes.bfloat16)).reshape(k // 32, 32, n)
    amax = np.abs(w).max(1)
    byte = np.clip(np.where(amax > 0, np.frexp(amax)[1] - 1 + 127 - 7, 1), 1, 254)
    scaled = (w * np.exp2(127.0 - byte)[:, None, :]).reshape(k, n).astype(np.float32)
    words = np.ascontiguousarray(scaled.reshape(k // 512, 128, 4, n).transpose(0, 1, 3, 2)).astype(ml_dtypes.float8_e4m3fn).view(np.uint8)
    return words, np.ascontiguousarray(byte.astype(np.uint8).reshape(k // 512, 16, n))


def unpack_weight(words, scales):
    g, p, n, _ = words.shape
    vals = np.ascontiguousarray(words).view(ml_dtypes.float8_e4m3fn).astype(np.float64) * np.repeat(np.exp2(scales.astype(np.float64) - 127.0), 8, axis=1)[..., None]
    return vals.transpose(0, 1, 3, 2).reshape(g * 512, n)


def gelu(v):
    return 0.5 * v * (1.0 + np.tanh(np.sqrt(2.0 / np.pi) * (v + 0.044715 * v**3)))


K, T, E, C, N = 2048, 512, 4, 256, 512


def by_expert(wq, xq):
    return np.concatenate([wq[e].T @ xq[:, e * C:(e + 1) * C] for e in range(E)], axis=1)


def setup_inputs():
    n = np.random.standard_normal
    s = mx_kscale(K)[:, None]
    first = np.random.permutation(np.repeat(np.arange(E), T // E))
    second = (first + 1 + np.random.permutation(np.repeat(np.arange(E - 1), -(-T // (E - 1)))[:T])) % E
    while np.bincount(second, minlength=E).max() != T // E:
        load = np.bincount(second, minlength=E); hi, lo = int(load.argmax()), int(load.argmin())
        t = np.flatnonzero((second == hi) & (first != lo))[0]; second[t] = lo
    slot_token = np.empty(E * C, np.int64); pos = np.empty((2, T), np.int64); fill = np.zeros(E, np.int64)
    place = np.stack([np.random.permutation(C) for _ in range(E)])
    for r, deal in enumerate((first, second)):
        for t in np.random.permutation(T):
            e = deal[t]; j = e * C + place[e, fill[e]]; fill[e] += 1; slot_token[j] = t; pos[r, t] = j
    g = np.random.uniform(0.2, 0.8, T)
    packed = [pack_weight(m) for m in n((E, K, N)) / np.sqrt(K) / s[None]]
    return {
        "xT": (n((K, T)) * s).astype(np.float32),
        "w_words": np.stack([m[0] for m in packed]),
        "w_scales": np.stack([m[1] for m in packed]),
        "b": (0.3 * n((N, E))).astype(np.float32),
        "gate": np.stack([np.tile(g, (N, 1)), np.tile(1.0 - g, (N, 1))]).astype(np.float32),
        "offs": striped(slot_token),
        "pos1": striped(pos[0]),
        "pos2": striped(pos[1]),
    }


def reference(xT, w_words, w_scales, b, gate, offs, pos1, pos2):
    idx = unstriped(offs)
    xq = mxq(f64(xT)[:, idx], 0, "e4m3")
    w = np.stack([unpack_weight(w_words[e], w_scales[e]) for e in range(E)])
    y = by_expert(w, xq)
    y = gelu(y + np.repeat(f64(b), C, axis=1))
    return f64(gate[0]) * y[:, unstriped(pos1)] + f64(gate[1]) * y[:, unstriped(pos2)]

@@ -1,0 +1,157 @@
+from contextlib import ExitStack
+
+import concourse.mybir as mybir
+
+K, T, E, C, N = 2048, 512, 4, 256, 512
+P = 128
+A = K // 512
+NB = N // P
+FLOPS = 2 * K * N * E * C
+
+F32 = mybir.dt.float32
+BF16 = mybir.dt.bfloat16
+U32 = mybir.dt.uint32
+I32 = mybir.dt.int32
+U16 = mybir.dt.uint16
+U8 = mybir.dt.uint8
+FP8X4 = mybir.dt.float8_e4m3fn_x4
+MULT = mybir.AluOpType.mult
+ADD = mybir.AluOpType.add
+GELU = mybir.ActivationFunctionType.Gelu_apprx_tanh
+
+
+def tile_routed_moe_kernel(tc, xT, w_words, w_scales, b, gate, offs, pos1, pos2, out):
+    nc = tc.nc
+    with ExitStack() as ctx:
+        keep = ctx.enter_context(tc.tile_pool(name="keep", bufs=1))
+        work = ctx.enter_context(tc.tile_pool(name="work", bufs=2))
+        psum = ctx.enter_context(tc.psum_pool(name="psum", bufs=1))
+
+        offs_sb = keep.tile([P, E * C // 16], U16, name="offs_sb")
+        pos1_sb = keep.tile([P, T // 16], U16, name="pos1_sb")
+        pos2_sb = keep.tile([P, T // 16], U16, name="pos2_sb")
+        raw = [keep.tile([P, 4, T], F32, name=f"raw{a}") for a in range(A)]
+        grouped = [keep.tile([P, T, 4], BF16, name=f"grouped{a}", align_bytes=64) for a in range(A)]
+        words = [keep.tile([P, T], U32, name=f"words{a}", align_bytes=64) for a in range(A)]
+        planes = keep.tile([P, T], U8, name="planes", align_bytes=64)
+        slot_words = [keep.tile([P, E * C], U32, name=f"slot_words{a}", align_bytes=64) for a in range(A)]
+        slot_planes = keep.tile([P, E * C], U8, name="slot_planes", align_bytes=64)
+        wq = keep.tile([P, E, A, N], U32, name="wq", align_bytes=64)
+        ws = keep.tile([P, E, A, N], U8, name="ws", align_bytes=64)
+        bias = keep.tile([P, NB, E], F32, name="bias")
+        gates = [keep.tile([P, 2, T], F32, name=f"gates{nb}") for nb in range(NB)]
+        y = [keep.tile([P, E * C], F32, name=f"y{nb}") for nb in range(NB)]
+        warm = keep.tile([P, 1], F32, name="warm")
+        banks = [[psum.tile([P, 512], F32, name=f"bank{nb}_{h}") for h in range(2)] for nb in range(NB)]
+
+        nc.gpsimd.memset(planes[:], 0)
+        nc.vector.memset(warm[:], 0.0)
+        nc.scalar.activation(warm[:], warm[:], GELU)
+        nc.vector.memset(ws[:].rearrange("p e a n -> p (e a n)").bitcast(I32), 0)
+
+        x = xT.rearrange("(a p t) n -> a p t n", p=P, t=4)
+        nc.sync.dma_start(offs_sb[:], offs)
+        for h in range(2):
+            cols = slice(h * 256, (h + 1) * 256)
+            nc.sync.dma_start(out=raw[0][:, :, cols], in_=x[0][:, :, cols])
+        for a in range(1, A):
+            nc.sync.dma_start(out=raw[a][:], in_=x[a])
+        for q in range(4):
+            nc.sync.dma_start(
+                out=ws[32 * q : 32 * q + 4, :, :, :].rearrange("i e a n -> i (e a) n").bitcast(I32),
+                in_=w_scales[:, :, 4 * q : 4 * q + 4, :].rearrange("e a i n -> i (e a) n").bitcast(I32),
+            )
+
+        nc.sync.dma_start(out=bias[:], in_=b.rearrange("(c p) e -> p c e", p=P))
+
+        def load_weights(half):
+            for e in range(E):
+                nc.sync.dma_start(
+                    out=wq[:, e, :, half * 256 : (half + 1) * 256].bitcast(I32),
+                    in_=w_words[e].rearrange("a p n r -> p a (n r)")[:, :, half * 1024 : (half + 1) * 1024].bitcast(I32),
+                )
+
+        def load_gate(nb):
+            nc.sync.dma_start(out=gates[nb][:], in_=gate.rearrange("r (c p) t -> c p r t", p=P)[nb])
+
+        load_weights(0)
+        nc.sync.dma_start(pos1_sb[:], pos1)
+        nc.sync.dma_start(pos2_sb[:], pos2)
+        load_gate(0)
+        load_gate(1)
+        load_weights(1)
+        load_gate(2)
+        load_gate(3)
+
+        def interleave(engine_copy, a, c0, c1):
+            engine_copy(
+                grouped[a][:, c0:c1, :].rearrange("p (c i) t -> p c t i", i=4),
+                raw[a][:, :, c0:c1].rearrange("p t (c i) -> p c t i", i=4),
+            )
+
+        def quantise(a, c0, c1):
+            nc.vector.quantize_mx(
+                out=words[a][:, c0:c1].bitcast(FP8X4),
+                scales=planes[4 * a : P, c0:c1],
+                in_=grouped[a][:, c0:c1, :].rearrange("p n t -> p (n t)"),
+            )
+
+        def gather_words(a, e):
+            nc.vector.tensor_copy(slot_words[a][:, e * C : (e + 1) * C], words[a][:].indirect(offs_sb[:, e * 16 : (e + 1) * 16]))
+
+        def gather_planes(e):
+            nc.vector.tensor_copy(slot_planes[:, e * C : (e + 1) * C], planes[:].indirect(offs_sb[:, e * 16 : (e + 1) * 16]))
+
+        for h in range(2):
+            c0 = h * 256
+            interleave(nc.vector.tensor_copy, 0, c0, c0 + 160)
+            interleave(nc.scalar.copy, 0, c0 + 160, c0 + 256)
+            quantise(0, c0, c0 + 256)
+        interleave(nc.scalar.copy, 1, 192, 512)
+        gather_words(0, 0)
+        gather_words(0, 1)
+        interleave(nc.vector.tensor_copy, 1, 0, 192)
+        gather_words(0, 2)
+        gather_words(0, 3)
+        quantise(1, 0, 512)
+        interleave(nc.scalar.copy, 2, 0, 512)
+        for e in range(E):
+            gather_words(1, e)
+        quantise(2, 0, 512)
+        interleave(nc.scalar.copy, 3, 0, 512)
+        gather_words(2, 0)
+        gather_words(2, 1)
+        quantise(3, 0, 512)
+
+        def expert(e, nbs):
+            for nb in nbs:
+                acc = banks[nb][e % 2][:, (e // 2) * C : (e // 2 + 1) * C]
+                for a in range(A):
+                    nc.tensor.matmul_mx(
+                        out=acc,
+                        lhsT=wq[:, e, a, nb * P : (nb + 1) * P].bitcast(FP8X4),
+                        lhsT_scale=ws[:, e, a, nb * P : (nb + 1) * P],
+                        rhs=slot_words[a][:, e * C : (e + 1) * C].bitcast(FP8X4),
+                        rhs_scale=slot_planes[4 * a : P, e * C : (e + 1) * C],
+                        start=(a == 0),
+                        stop=(a == A - 1),
+                    )
+                nc.scalar.activation(y[nb][:, e * C : (e + 1) * C], acc, GELU, bias=bias[:, nb, e : e + 1])
+
+        for e in range(E):
+            gather_planes(e)
+            if e >= 2:
+                gather_words(2, e)
+            gather_words(3, e)
+            expert(e, (0, 1))
+        for e in range(E):
+            expert(e, (2, 3))
+
+        for nb in range(NB):
+            first = work.tile([P, T], F32, name="first")
+            second = work.tile([P, T], F32, name="second")
+            total = work.tile([P, T], F32, name="total")
+            nc.vector.tensor_tensor(first[:], y[nb][:].indirect(pos1_sb[:]), gates[nb][:, 0, :], MULT)
+            nc.vector.tensor_tensor(second[:], y[nb][:].indirect(pos2_sb[:]), gates[nb][:, 1, :], MULT)
+            nc.vector.tensor_tensor(total[:], first[:], second[:], ADD)
+            nc.sync.dma_start(out=out[nb * P : (nb + 1) * P, :], in_=total[:])

@@ -1,11 +1,13 @@
 from contextlib import ExitStack
 
 import concourse.mybir as mybir
+from concourse.masks import make_identity
 
 K, T, E, C, N = 2048, 512, 4, 256, 512
 P = 128
 A = K // 512
 NB = N // P
+PAD = 896
 FLOPS = 2 * K * N * E * C
 
 F32 = mybir.dt.float32
@@ -24,7 +26,7 @@ def tile_routed_moe_kernel(tc, xT, w_words, w_scales, b, gate, offs, pos1, pos2,
     nc = tc.nc
     with ExitStack() as ctx:
         keep = ctx.enter_context(tc.tile_pool(name="keep", bufs=1))
-        work = ctx.enter_context(tc.tile_pool(name="work", bufs=2))
+        work = ctx.enter_context(tc.tile_pool(name="work", bufs=4))
         psum = ctx.enter_context(tc.psum_pool(name="psum", bufs=1))
 
         offs_sb = keep.tile([P, E * C // 16], U16, name="offs_sb")
@@ -32,54 +34,67 @@ def tile_routed_moe_kernel(tc, xT, w_words, w_scales, b, gate, offs, pos1, pos2,
         pos2_sb = keep.tile([P, T // 16], U16, name="pos2_sb")
         raw = [keep.tile([P, 4, T], F32, name=f"raw{a}") for a in range(A)]
         grouped = [keep.tile([P, T, 4], BF16, name=f"grouped{a}", align_bytes=64) for a in range(A)]
-        words = [keep.tile([P, T], U32, name=f"words{a}", align_bytes=64) for a in range(A)]
-        planes = keep.tile([P, T], U8, name="planes", align_bytes=64)
+        words = keep.tile([P, A * T + PAD], I32, name="words", align_bytes=64)
+        planes = keep.tile([P, T + 192], U8, name="planes", align_bytes=64)
         slot_words = [keep.tile([P, E * C], U32, name=f"slot_words{a}", align_bytes=64) for a in range(A)]
         slot_planes = keep.tile([P, E * C], U8, name="slot_planes", align_bytes=64)
         wq = keep.tile([P, E, A, N], U32, name="wq", align_bytes=64)
-        ws = keep.tile([P, E, A, N], U8, name="ws", align_bytes=64)
+        ws = keep.tile([P, E, N], U8, name="ws", align_bytes=64)
         bias = keep.tile([P, NB, E], F32, name="bias")
         gates = [keep.tile([P, 2, T], F32, name=f"gates{nb}") for nb in range(NB)]
         y = [keep.tile([P, E * C], F32, name=f"y{nb}") for nb in range(NB)]
         warm = keep.tile([P, 1], F32, name="warm")
-        banks = [[psum.tile([P, 512], F32, name=f"bank{nb}_{h}") for h in range(2)] for nb in range(NB)]
 
         nc.gpsimd.memset(planes[:], 0)
         nc.vector.memset(warm[:], 0.0)
         nc.scalar.activation(warm[:], warm[:], GELU)
-        nc.vector.memset(ws[:].rearrange("p e a n -> p (e a n)").bitcast(I32), 0)
+        nc.vector.memset(ws[:].rearrange("p e n -> p (e n)").bitcast(I32), 0)
+        nc.vector.memset(words[:, A * T :], 0)
+        ident = keep.tile([P, P], F32, name="ident")
+        make_identity(nc, ident[:])
 
         x = xT.rearrange("(a p t) n -> a p t n", p=P, t=4)
-        nc.sync.dma_start(offs_sb[:], offs)
-        for h in range(2):
-            cols = slice(h * 256, (h + 1) * 256)
-            nc.sync.dma_start(out=raw[0][:, :, cols], in_=x[0][:, :, cols])
-        for a in range(1, A):
-            nc.sync.dma_start(out=raw[a][:], in_=x[a])
-        for q in range(4):
-            nc.sync.dma_start(
-                out=ws[32 * q : 32 * q + 4, :, :, :].rearrange("i e a n -> i (e a) n").bitcast(I32),
-                in_=w_scales[:, :, 4 * q : 4 * q + 4, :].rearrange("e a i n -> i (e a) n").bitcast(I32),
-            )
 
-        nc.sync.dma_start(out=bias[:], in_=b.rearrange("(c p) e -> p c e", p=P))
-
-        def load_weights(half):
-            for e in range(E):
+        def load_scales(e):
+            for q in range(4):
                 nc.sync.dma_start(
-                    out=wq[:, e, :, half * 256 : (half + 1) * 256].bitcast(I32),
-                    in_=w_words[e].rearrange("a p n r -> p a (n r)")[:, :, half * 1024 : (half + 1) * 1024].bitcast(I32),
+                    out=ws[32 * q : 32 * q + 16, e, :].bitcast(I32),
+                    in_=w_scales[e, :, 4 * q : 4 * q + 4, :].bitcast(I32),
                 )
+
+        def load_weights(e, half):
+            nc.sync.dma_start(
+                out=wq[:, e, :, half * 256 : (half + 1) * 256].bitcast(I32),
+                in_=w_words[e].rearrange("a p n r -> p a (n r)")[:, :, half * 1024 : (half + 1) * 1024].bitcast(I32),
+            )
 
         def load_gate(nb):
             nc.sync.dma_start(out=gates[nb][:], in_=gate.rearrange("r (c p) t -> c p r t", p=P)[nb])
 
-        load_weights(0)
+        for h in range(2):
+            cols = slice(h * 256, (h + 1) * 256)
+            nc.sync.dma_start(out=raw[3][:, :, cols], in_=x[3][:, :, cols])
+        nc.sync.dma_start(offs_sb[:], offs)
+        nc.sync.dma_start(out=raw[2][:], in_=x[2])
+        load_scales(0)
+        nc.sync.dma_start(out=raw[1][:], in_=x[1])
+        load_scales(1)
+        nc.sync.dma_start(out=raw[0][:], in_=x[0])
+        nc.sync.dma_start(out=bias[:], in_=b.rearrange("(c p) e -> p c e", p=P))
+        load_scales(2)
+        load_weights(0, 0)
+        load_weights(1, 0)
+        load_scales(3)
+        load_weights(2, 0)
+        load_weights(3, 0)
         nc.sync.dma_start(pos1_sb[:], pos1)
         nc.sync.dma_start(pos2_sb[:], pos2)
         load_gate(0)
+        load_weights(0, 1)
+        load_weights(1, 1)
         load_gate(1)
-        load_weights(1)
+        load_weights(2, 1)
+        load_weights(3, 1)
         load_gate(2)
         load_gate(3)
 
@@ -91,67 +106,97 @@ def tile_routed_moe_kernel(tc, xT, w_words, w_scales, b, gate, offs, pos1, pos2,
 
         def quantise(a, c0, c1):
             nc.vector.quantize_mx(
-                out=words[a][:, c0:c1].bitcast(FP8X4),
+                out=words[:, a * T + c0 : a * T + c1].bitcast(FP8X4),
                 scales=planes[4 * a : P, c0:c1],
                 in_=grouped[a][:, c0:c1, :].rearrange("p n t -> p (n t)"),
             )
 
-        def gather_words(a, e):
-            nc.vector.tensor_copy(slot_words[a][:, e * C : (e + 1) * C], words[a][:].indirect(offs_sb[:, e * 16 : (e + 1) * 16]))
+        def gather_words(a, s0, s1):
+            window = words[:, a * T : (a + 1) * T + PAD].bitcast(U32)
+            nc.vector.tensor_copy(slot_words[a][:, s0:s1], window.indirect(offs_sb[:, s0 // 16 : s1 // 16]))
 
-        def gather_planes(e):
-            nc.vector.tensor_copy(slot_planes[:, e * C : (e + 1) * C], planes[:].indirect(offs_sb[:, e * 16 : (e + 1) * 16]))
+        def gather_planes(s0, s1):
+            nc.vector.tensor_copy(slot_planes[:, s0:s1], planes[:].indirect(offs_sb[:, s0 // 16 : s1 // 16]))
 
         for h in range(2):
             c0 = h * 256
-            interleave(nc.vector.tensor_copy, 0, c0, c0 + 160)
-            interleave(nc.scalar.copy, 0, c0 + 160, c0 + 256)
-            quantise(0, c0, c0 + 256)
-        interleave(nc.scalar.copy, 1, 192, 512)
-        gather_words(0, 0)
-        gather_words(0, 1)
-        interleave(nc.vector.tensor_copy, 1, 0, 192)
-        gather_words(0, 2)
-        gather_words(0, 3)
-        quantise(1, 0, 512)
-        interleave(nc.scalar.copy, 2, 0, 512)
-        for e in range(E):
-            gather_words(1, e)
+            interleave(nc.vector.tensor_copy, 3, c0, c0 + 160)
+            interleave(nc.scalar.copy, 3, c0 + 160, c0 + 256)
+            quantise(3, c0, c0 + 256)
+        interleave(nc.scalar.copy, 2, 192, 512)
+        gather_words(3, 0, 1024)
+
+        interleave(nc.vector.tensor_copy, 2, 0, 192)
         quantise(2, 0, 512)
-        interleave(nc.scalar.copy, 3, 0, 512)
-        gather_words(2, 0)
-        gather_words(2, 1)
-        quantise(3, 0, 512)
+        interleave(nc.scalar.copy, 1, 0, 512)
+        gather_words(2, 0, 1024)
+        quantise(1, 0, 512)
+        interleave(nc.scalar.copy, 0, 0, 512)
+        gather_words(1, 0, 1024)
+        quantise(0, 0, 512)
 
-        def expert(e, nbs):
-            for nb in nbs:
-                acc = banks[nb][e % 2][:, (e // 2) * C : (e // 2 + 1) * C]
-                for a in range(A):
-                    nc.tensor.matmul_mx(
-                        out=acc,
-                        lhsT=wq[:, e, a, nb * P : (nb + 1) * P].bitcast(FP8X4),
-                        lhsT_scale=ws[:, e, a, nb * P : (nb + 1) * P],
-                        rhs=slot_words[a][:, e * C : (e + 1) * C].bitcast(FP8X4),
-                        rhs_scale=slot_planes[4 * a : P, e * C : (e + 1) * C],
-                        start=(a == 0),
-                        stop=(a == A - 1),
-                    )
-                nc.scalar.activation(y[nb][:, e * C : (e + 1) * C], acc, GELU, bias=bias[:, nb, e : e + 1])
+        for s0 in range(0, E * C, 512):
+            gather_planes(s0, s0 + 512)
+        gather_words(0, 0, 512)
+        gather_words(0, 512, 1024)
 
+        def slots(e):
+            return slice(e * C, (e + 1) * C)
+
+        def multiply(acc, nb, e, a):
+            nc.tensor.matmul_mx(
+                out=acc[:],
+                lhsT=wq[:, e, a, nb * P : (nb + 1) * P].bitcast(FP8X4),
+                lhsT_scale=ws[4 * a : P, e, nb * P : (nb + 1) * P],
+                rhs=slot_words[a][:, slots(e)].bitcast(FP8X4),
+                rhs_scale=slot_planes[4 * a : P, slots(e)],
+                start=(a == 3),
+                stop=(a == 0),
+            )
+
+        def activate(acc, nb, e):
+            nc.scalar.activation(y[nb][:, slots(e)], acc[:], GELU, bias=bias[:, nb, e : e + 1])
+
+        accs = [psum.tile([P, C], F32, name=f"acc0_{e}", tag="acc", bufs=6) for e in range(E)]
+        for a in (3, 2, 1, 0):
+            for e in range(E):
+                multiply(accs[e], 0, e, a)
         for e in range(E):
-            gather_planes(e)
-            if e >= 2:
-                gather_words(2, e)
-            gather_words(3, e)
-            expert(e, (0, 1))
-        for e in range(E):
-            expert(e, (2, 3))
+            activate(accs[e], 0, e)
+        for nb in range(1, NB):
+            for e in range(E):
+                acc = psum.tile([P, C], F32, name=f"acc{nb}_{e}", tag="acc" if (nb, e) != (3, 3) else "last", bufs=6 if (nb, e) != (3, 3) else 1)
+                for a in (3, 2, 1, 0):
+                    multiply(acc, nb, e, a)
+                activate(acc, nb, e)
+
+        first = [None] * NB
+        second = [None] * NB
+
+        def products(nb):
+            first[nb] = work.tile([P, T], F32, name="first")
+            second[nb] = work.tile([P, T], F32, name="second")
+            nc.vector.tensor_tensor(first[nb][:], y[nb][:].indirect(pos1_sb[:]), gates[nb][:, 0, :], MULT)
+            nc.vector.tensor_tensor(second[nb][:], y[nb][:].indirect(pos2_sb[:]), gates[nb][:, 1, :], MULT)
+
+        def add_and_store(nb):
+            total = work.tile([P, T], F32, name="total")
+            if nb < 1:
+                acc = psum.tile([P, T], F32, name=f"both{nb}", tag="last", bufs=1)
+                nc.tensor.matmul(acc[:], ident[:], first[nb][:], start=True, stop=False)
+                nc.tensor.matmul(acc[:], ident[:], second[nb][:], start=False, stop=True)
+                nc.scalar.copy(total[:], acc[:])
+            elif nb < NB - 1:
+                nc.vector.tensor_tensor(total[:], first[nb][:], second[nb][:], ADD)
+            else:
+                for cols in (slice(0, 256), slice(256, 512)):
+                    nc.vector.tensor_tensor(total[:, cols], first[nb][:, cols], second[nb][:, cols], ADD)
+                    nc.sync.dma_start(out=out[nb * P : (nb + 1) * P, cols], in_=total[:, cols])
+                return
+            nc.sync.dma_start(out=out[nb * P : (nb + 1) * P, :], in_=total[:])
 
         for nb in range(NB):
-            first = work.tile([P, T], F32, name="first")
-            second = work.tile([P, T], F32, name="second")
-            total = work.tile([P, T], F32, name="total")
-            nc.vector.tensor_tensor(first[:], y[nb][:].indirect(pos1_sb[:]), gates[nb][:, 0, :], MULT)
-            nc.vector.tensor_tensor(second[:], y[nb][:].indirect(pos2_sb[:]), gates[nb][:, 1, :], MULT)
-            nc.vector.tensor_tensor(total[:], first[:], second[:], ADD)
-            nc.sync.dma_start(out=out[nb * P : (nb + 1) * P, :], in_=total[:])
+            products(nb)
+            if nb > 0:
+                add_and_store(nb - 1)
+        add_and_store(NB - 1)

@@ -8,6 +8,7 @@ P = 128
 A = K // 512
 NB = N // P
 PAD = 896
+TENSOR_ADD = (512, 256, 0, 0)
 FLOPS = 2 * K * N * E * C
 
 F32 = mybir.dt.float32
@@ -80,10 +81,10 @@ def tile_routed_moe_kernel(tc, xT, w_words, w_scales, b, gate, offs, pos1, pos2,
         nc.sync.dma_start(out=raw[1][:], in_=x[1])
         load_scales(1)
         nc.sync.dma_start(out=raw[0][:], in_=x[0])
-        nc.sync.dma_start(out=bias[:], in_=b.rearrange("(c p) e -> p c e", p=P))
         load_scales(2)
         load_weights(0, 0)
         load_weights(1, 0)
+        nc.sync.dma_start(out=bias[:], in_=b.rearrange("(c p) e -> p c e", p=P))
         load_scales(3)
         load_weights(2, 0)
         load_weights(3, 0)
@@ -120,8 +121,8 @@ def tile_routed_moe_kernel(tc, xT, w_words, w_scales, b, gate, offs, pos1, pos2,
 
         for h in range(2):
             c0 = h * 256
-            interleave(nc.vector.tensor_copy, 3, c0, c0 + 160)
-            interleave(nc.scalar.copy, 3, c0 + 160, c0 + 256)
+            interleave(nc.vector.tensor_copy, 3, c0, c0 + 192)
+            interleave(nc.scalar.copy, 3, c0 + 192, c0 + 256)
             quantise(3, c0, c0 + 256)
         interleave(nc.scalar.copy, 2, 192, 512)
         gather_words(3, 0, 1024)
@@ -129,16 +130,18 @@ def tile_routed_moe_kernel(tc, xT, w_words, w_scales, b, gate, offs, pos1, pos2,
         interleave(nc.vector.tensor_copy, 2, 0, 192)
         quantise(2, 0, 512)
         interleave(nc.scalar.copy, 1, 0, 512)
-        gather_words(2, 0, 1024)
+        gather_words(2, 0, 768)
         quantise(1, 0, 512)
+        gather_words(2, 768, 1024)
         interleave(nc.scalar.copy, 0, 0, 512)
-        gather_words(1, 0, 1024)
+        gather_words(1, 0, 768)
         quantise(0, 0, 512)
-
-        for s0 in range(0, E * C, 512):
-            gather_planes(s0, s0 + 512)
+        gather_words(1, 768, 1024)
+        gather_planes(0, 512)
         gather_words(0, 0, 512)
-        gather_words(0, 512, 1024)
+        gather_planes(512, 1024)
+        gather_words(0, 512, 768)
+        gather_words(0, 768, 1024)
 
         def slots(e):
             return slice(e * C, (e + 1) * C)
@@ -165,7 +168,8 @@ def tile_routed_moe_kernel(tc, xT, w_words, w_scales, b, gate, offs, pos1, pos2,
             activate(accs[e], 0, e)
         for nb in range(1, NB):
             for e in range(E):
-                acc = psum.tile([P, C], F32, name=f"acc{nb}_{e}", tag="acc" if (nb, e) != (3, 3) else "last", bufs=6 if (nb, e) != (3, 3) else 1)
+                last = nb == NB - 1 and e >= 2
+                acc = psum.tile([P, C], F32, name=f"acc{nb}_{e}", tag=f"sum{e - 2}" if last else "acc", bufs=1 if last else 6)
                 for a in (3, 2, 1, 0):
                     multiply(acc, nb, e, a)
                 activate(acc, nb, e)
@@ -181,19 +185,23 @@ def tile_routed_moe_kernel(tc, xT, w_words, w_scales, b, gate, offs, pos1, pos2,
 
         def add_and_store(nb):
             total = work.tile([P, T], F32, name="total")
-            if nb < 1:
-                acc = psum.tile([P, T], F32, name=f"both{nb}", tag="last", bufs=1)
-                nc.tensor.matmul(acc[:], ident[:], first[nb][:], start=True, stop=False)
-                nc.tensor.matmul(acc[:], ident[:], second[nb][:], start=False, stop=True)
-                nc.scalar.copy(total[:], acc[:])
-            elif nb < NB - 1:
-                nc.vector.tensor_tensor(total[:], first[nb][:], second[nb][:], ADD)
-            else:
-                for cols in (slice(0, 256), slice(256, 512)):
+            split = TENSOR_ADD[nb]
+            if split > 0:
+                acc = psum.tile([P, split], F32, name=f"sum_{nb}", tag=f"sum{nb}", bufs=1)
+                nc.tensor.matmul(acc[:], ident[:], first[nb][:, :split], start=True, stop=False)
+                nc.tensor.matmul(acc[:], ident[:], second[nb][:, :split], start=False, stop=True)
+                nc.scalar.copy(total[:, :split], acc[:])
+            ends = (384, T) if nb == NB - 1 else (T,)
+            start = split
+            for end in ends:
+                if end > start:
+                    cols = slice(start, end)
                     nc.vector.tensor_tensor(total[:, cols], first[nb][:, cols], second[nb][:, cols], ADD)
+                if nb == NB - 1:
                     nc.sync.dma_start(out=out[nb * P : (nb + 1) * P, cols], in_=total[:, cols])
-                return
-            nc.sync.dma_start(out=out[nb * P : (nb + 1) * P, :], in_=total[:])
+                start = end
+            if nb < NB - 1:
+                nc.sync.dma_start(out=out[nb * P : (nb + 1) * P, :], in_=total[:])
 
         for nb in range(NB):
             products(nb)

@@ -63,10 +63,10 @@ def tile_routed_moe_kernel(tc, xT, w_words, w_scales, b, gate, offs, pos1, pos2,
                     in_=w_scales[e, :, 4 * q : 4 * q + 4, :].bitcast(I32),
                 )
 
-        def load_weights(e, half):
+        def load_weights(e, n0, n1):
             nc.sync.dma_start(
-                out=wq[:, e, :, half * 256 : (half + 1) * 256].bitcast(I32),
-                in_=w_words[e].rearrange("a p n r -> p a (n r)")[:, :, half * 1024 : (half + 1) * 1024].bitcast(I32),
+                out=wq[:, e, :, n0:n1].bitcast(I32),
+                in_=w_words[e].rearrange("a p n r -> p a (n r)")[:, :, 4 * n0 : 4 * n1].bitcast(I32),
             )
 
         def load_gate(nb):
@@ -82,20 +82,18 @@ def tile_routed_moe_kernel(tc, xT, w_words, w_scales, b, gate, offs, pos1, pos2,
         load_scales(1)
         nc.sync.dma_start(out=raw[0][:], in_=x[0])
         load_scales(2)
-        load_weights(0, 0)
-        load_weights(1, 0)
+        load_weights(0, 0, N)
+        load_weights(1, 0, N)
         nc.sync.dma_start(out=bias[:], in_=b.rearrange("(c p) e -> p c e", p=P))
         load_scales(3)
-        load_weights(2, 0)
-        load_weights(3, 0)
+        load_weights(2, 0, N // 2)
+        load_weights(3, 0, N // 2)
         nc.sync.dma_start(pos1_sb[:], pos1)
         nc.sync.dma_start(pos2_sb[:], pos2)
         load_gate(0)
-        load_weights(0, 1)
-        load_weights(1, 1)
         load_gate(1)
-        load_weights(2, 1)
-        load_weights(3, 1)
+        load_weights(2, N // 2, N)
+        load_weights(3, N // 2, N)
         load_gate(2)
         load_gate(3)
 

from contextlib import ExitStack

import concourse.mybir as mybir
from concourse.masks import make_identity

K, T, E, C, N = 2048, 512, 4, 256, 512
P = 128
A = K // 512
NB = N // P
PAD = 896
TENSOR_ADD = (512, 256, 0, 0)
FLOPS = 2 * K * N * E * C

F32 = mybir.dt.float32
BF16 = mybir.dt.bfloat16
U32 = mybir.dt.uint32
I32 = mybir.dt.int32
U16 = mybir.dt.uint16
U8 = mybir.dt.uint8
FP8X4 = mybir.dt.float8_e4m3fn_x4
MULT = mybir.AluOpType.mult
ADD = mybir.AluOpType.add
GELU = mybir.ActivationFunctionType.Gelu_apprx_tanh


def tile_routed_moe_kernel(tc, xT, w_words, w_scales, b, gate, offs, pos1, pos2, out):
    nc = tc.nc
    with ExitStack() as ctx:
        keep = ctx.enter_context(tc.tile_pool(name="keep", bufs=1))
        work = ctx.enter_context(tc.tile_pool(name="work", bufs=4))
        psum = ctx.enter_context(tc.psum_pool(name="psum", bufs=1))

        offs_sb = keep.tile([P, E * C // 16], U16, name="offs_sb")
        pos1_sb = keep.tile([P, T // 16], U16, name="pos1_sb")
        pos2_sb = keep.tile([P, T // 16], U16, name="pos2_sb")
        raw = [keep.tile([P, 4, T], F32, name=f"raw{a}") for a in range(A)]
        grouped = [keep.tile([P, T, 4], BF16, name=f"grouped{a}", align_bytes=64) for a in range(A)]
        words = keep.tile([P, A * T + PAD], I32, name="words", align_bytes=64)
        planes = keep.tile([P, T + 192], U8, name="planes", align_bytes=64)
        slot_words = [keep.tile([P, E * C], U32, name=f"slot_words{a}", align_bytes=64) for a in range(A)]
        slot_planes = keep.tile([P, E * C], U8, name="slot_planes", align_bytes=64)
        wq = keep.tile([P, E, A, N], U32, name="wq", align_bytes=64)
        ws = keep.tile([P, E, N], U8, name="ws", align_bytes=64)
        bias = keep.tile([P, NB, E], F32, name="bias")
        gates = [keep.tile([P, 2, T], F32, name=f"gates{nb}") for nb in range(NB)]
        y = [keep.tile([P, E * C], F32, name=f"y{nb}") for nb in range(NB)]
        warm = keep.tile([P, 1], F32, name="warm")

        nc.gpsimd.memset(planes[:], 0)
        nc.vector.memset(warm[:], 0.0)
        nc.scalar.activation(warm[:], warm[:], GELU)
        nc.vector.memset(ws[:].rearrange("p e n -> p (e n)").bitcast(I32), 0)
        nc.vector.memset(words[:, A * T :], 0)
        ident = keep.tile([P, P], F32, name="ident")
        make_identity(nc, ident[:])

        x = xT.rearrange("(a p t) n -> a p t n", p=P, t=4)

        def load_scales(e):
            for q in range(4):
                nc.sync.dma_start(
                    out=ws[32 * q : 32 * q + 16, e, :].bitcast(I32),
                    in_=w_scales[e, :, 4 * q : 4 * q + 4, :].bitcast(I32),
                )

        def load_weights(e, n0, n1):
            nc.sync.dma_start(
                out=wq[:, e, :, n0:n1].bitcast(I32),
                in_=w_words[e].rearrange("a p n r -> p a (n r)")[:, :, 4 * n0 : 4 * n1].bitcast(I32),
            )

        def load_gate(nb):
            nc.sync.dma_start(out=gates[nb][:], in_=gate.rearrange("r (c p) t -> c p r t", p=P)[nb])

        for h in range(2):
            cols = slice(h * 256, (h + 1) * 256)
            nc.sync.dma_start(out=raw[3][:, :, cols], in_=x[3][:, :, cols])
        nc.sync.dma_start(offs_sb[:], offs)
        nc.sync.dma_start(out=raw[2][:], in_=x[2])
        load_scales(0)
        nc.sync.dma_start(out=raw[1][:], in_=x[1])
        load_scales(1)
        nc.sync.dma_start(out=raw[0][:], in_=x[0])
        load_scales(2)
        load_weights(0, 0, N)
        load_weights(1, 0, N)
        nc.sync.dma_start(out=bias[:], in_=b.rearrange("(c p) e -> p c e", p=P))
        load_scales(3)
        load_weights(2, 0, N // 2)
        load_weights(3, 0, N // 2)
        nc.sync.dma_start(pos1_sb[:], pos1)
        nc.sync.dma_start(pos2_sb[:], pos2)
        load_gate(0)
        load_gate(1)
        load_weights(2, N // 2, N)
        load_weights(3, N // 2, N)
        load_gate(2)
        load_gate(3)

        def interleave(engine_copy, a, c0, c1):
            engine_copy(
                grouped[a][:, c0:c1, :].rearrange("p (c i) t -> p c t i", i=4),
                raw[a][:, :, c0:c1].rearrange("p t (c i) -> p c t i", i=4),
            )

        def quantise(a, c0, c1):
            nc.vector.quantize_mx(
                out=words[:, a * T + c0 : a * T + c1].bitcast(FP8X4),
                scales=planes[4 * a : P, c0:c1],
                in_=grouped[a][:, c0:c1, :].rearrange("p n t -> p (n t)"),
            )

        def gather_words(a, s0, s1):
            window = words[:, a * T : (a + 1) * T + PAD].bitcast(U32)
            nc.vector.tensor_copy(slot_words[a][:, s0:s1], window.indirect(offs_sb[:, s0 // 16 : s1 // 16]))

        def gather_planes(s0, s1):
            nc.vector.tensor_copy(slot_planes[:, s0:s1], planes[:].indirect(offs_sb[:, s0 // 16 : s1 // 16]))

        for h in range(2):
            c0 = h * 256
            interleave(nc.vector.tensor_copy, 3, c0, c0 + 192)
            interleave(nc.scalar.copy, 3, c0 + 192, c0 + 256)
            quantise(3, c0, c0 + 256)
        interleave(nc.scalar.copy, 2, 192, 512)
        gather_words(3, 0, 1024)

        interleave(nc.vector.tensor_copy, 2, 0, 192)
        quantise(2, 0, 512)
        interleave(nc.scalar.copy, 1, 0, 512)
        gather_words(2, 0, 768)
        quantise(1, 0, 512)
        gather_words(2, 768, 1024)
        interleave(nc.scalar.copy, 0, 0, 512)
        gather_words(1, 0, 768)
        quantise(0, 0, 512)
        gather_words(1, 768, 1024)
        gather_planes(0, 512)
        gather_words(0, 0, 512)
        gather_planes(512, 1024)
        gather_words(0, 512, 768)
        gather_words(0, 768, 1024)

        def slots(e):
            return slice(e * C, (e + 1) * C)

        def multiply(acc, nb, e, a):
            nc.tensor.matmul_mx(
                out=acc[:],
                lhsT=wq[:, e, a, nb * P : (nb + 1) * P].bitcast(FP8X4),
                lhsT_scale=ws[4 * a : P, e, nb * P : (nb + 1) * P],
                rhs=slot_words[a][:, slots(e)].bitcast(FP8X4),
                rhs_scale=slot_planes[4 * a : P, slots(e)],
                start=(a == 3),
                stop=(a == 0),
            )

        def activate(acc, nb, e):
            nc.scalar.activation(y[nb][:, slots(e)], acc[:], GELU, bias=bias[:, nb, e : e + 1])

        accs = [psum.tile([P, C], F32, name=f"acc0_{e}", tag="acc", bufs=6) for e in range(E)]
        for a in (3, 2, 1, 0):
            for e in range(E):
                multiply(accs[e], 0, e, a)
        for e in range(E):
            activate(accs[e], 0, e)
        for nb in range(1, NB):
            for e in range(E):
                last = nb == NB - 1 and e >= 2
                acc = psum.tile([P, C], F32, name=f"acc{nb}_{e}", tag=f"sum{e - 2}" if last else "acc", bufs=1 if last else 6)
                for a in (3, 2, 1, 0):
                    multiply(acc, nb, e, a)
                activate(acc, nb, e)

        first = [None] * NB
        second = [None] * NB

        def products(nb):
            first[nb] = work.tile([P, T], F32, name="first")
            second[nb] = work.tile([P, T], F32, name="second")
            nc.vector.tensor_tensor(first[nb][:], y[nb][:].indirect(pos1_sb[:]), gates[nb][:, 0, :], MULT)
            nc.vector.tensor_tensor(second[nb][:], y[nb][:].indirect(pos2_sb[:]), gates[nb][:, 1, :], MULT)

        def add_and_store(nb):
            total = work.tile([P, T], F32, name="total")
            split = TENSOR_ADD[nb]
            if split > 0:
                acc = psum.tile([P, split], F32, name=f"sum_{nb}", tag=f"sum{nb}", bufs=1)
                nc.tensor.matmul(acc[:], ident[:], first[nb][:, :split], start=True, stop=False)
                nc.tensor.matmul(acc[:], ident[:], second[nb][:, :split], start=False, stop=True)
                nc.scalar.copy(total[:, :split], acc[:])
            ends = (384, T) if nb == NB - 1 else (T,)
            start = split
            for end in ends:
                if end > start:
                    cols = slice(start, end)
                    nc.vector.tensor_tensor(total[:, cols], first[nb][:, cols], second[nb][:, cols], ADD)
                if nb == NB - 1:
                    nc.sync.dma_start(out=out[nb * P : (nb + 1) * P, cols], in_=total[:, cols])
                start = end
            if nb < NB - 1:
                nc.sync.dma_start(out=out[nb * P : (nb + 1) * P, :], in_=total[:])

        for nb in range(NB):
            products(nb)
            if nb > 0:
                add_and_store(nb - 1)
        add_and_store(NB - 1)
